import numpy as np
import ml_dtypes

BF16 = ml_dtypes.bfloat16


def bf(x):
    return np.asarray(x, np.float32).astype(BF16)


def f32(x):
    return np.asarray(x, np.float32)


def f64(x):
    return np.asarray(x).astype(np.float64)


def striped(idx):
    return np.tile(idx.reshape(-1, 16).T, (8, 1))


A, S, K, M, N, E, Q = 256, 512, 256, 128, 256, 4, 64


def setup_inputs():
    return {"a": bf(np.random.standard_normal((A, S))), "wd": bf(np.random.standard_normal((A, M)) / np.sqrt(A)), "x": bf(np.random.standard_normal((K, N))), "w": bf(1.2 * np.random.standard_normal((E, K, M)) / np.sqrt(K)), "s": f32(0.5 + np.random.random_sample((M, 1))), "offs": striped(np.random.permutation(S)[:N])}


def reference(a, wd, x, w, s, offs):
    idx = offs[:16].T.reshape(-1)
    z = f64(wd).T @ f64(a)
    for e in range(E):
        z[:, idx[e * Q : (e + 1) * Q]] += f64(w)[e].T @ f64(x)[:, e * Q : (e + 1) * Q]
    z = z / np.sqrt((z**2).mean(axis=0, keepdims=True) + 1e-5) * f64(s)
    return z

@@ -1,0 +1,66 @@
+import concourse.mybir as mybir
+
+BF16, F32, U16 = mybir.dt.bfloat16, mybir.dt.float32, mybir.dt.uint16
+Act = mybir.ActivationFunctionType
+mult = mybir.AluOpType.mult
+
+P = 128
+BLOCKS = 2
+TOKENS = 512
+EXPERTS = 4
+PIECE = 64
+ENTRIES = EXPERTS * PIECE
+EPS = 1e-5
+
+FLOPS = 2 * BLOCKS * P * P * (TOKENS + ENTRIES) + 4 * P * TOKENS
+
+
+def tile_rows_placenorm_proj_kernel(tc, a, wd, x, w, s, offs, out):
+    nc = tc.nc
+    with (
+        tc.tile_pool(name="held", bufs=1) as held,
+        tc.psum_pool(name="psum", bufs=1) as psum,
+    ):
+        a_tile = held.tile([P, BLOCKS, TOKENS], BF16)
+        wd_tile = held.tile([P, BLOCKS, P], BF16)
+        x_tile = held.tile([P, BLOCKS, ENTRIES], BF16)
+        w_tile = held.tile([P, EXPERTS, BLOCKS, P], BF16)
+        gain = held.tile([P, 1], F32)
+        offsets = held.tile([P, ENTRIES // 16], U16)
+
+        nc.sync.dma_start(a_tile[:], a.rearrange("(p b) i -> p b i", b=BLOCKS))
+        nc.scalar.dma_start(wd_tile[:], wd.rearrange("(p b) m -> p b m", b=BLOCKS))
+        nc.sync.dma_start(offsets[:], offs)
+        nc.scalar.dma_start(w_tile[:], w.rearrange("e (p b) m -> p e b m", b=BLOCKS))
+        nc.sync.dma_start(x_tile[:], x.rearrange("(p b) j -> p b j", b=BLOCKS))
+        nc.scalar.dma_start(gain[:], s)
+
+        mean_weights = held.tile([P, P], BF16)
+        nc.vector.memset(mean_weights[:], 1.0 / P)
+        eps = held.tile([P, 1], F32)
+        nc.vector.memset(eps[:], EPS)
+
+        window = psum.tile([P, TOKENS], F32)
+        for b in range(BLOCKS):
+            nc.tensor.matmul(window[:], wd_tile[:, b, :], a_tile[:, b, :], start=(b == 0), stop=False)
+
+        for e in range(EXPERTS):
+            placed = window[:].indirect(offsets[:, e * PIECE // 16 : (e + 1) * PIECE // 16])
+            for b in range(BLOCKS):
+                nc.tensor.matmul(
+                    placed,
+                    w_tile[:, e, b, :],
+                    x_tile[:, b, e * PIECE : (e + 1) * PIECE],
+                    start=False,
+                    stop=(e == EXPERTS - 1 and b == BLOCKS - 1),
+                )
+
+        squares = held.tile([P, TOKENS], BF16)
+        mean_square = psum.tile([P, TOKENS], F32)
+        inverse_rms = held.tile([P, TOKENS], F32)
+        result = held.tile([P, TOKENS], F32)
+        nc.scalar.activation(squares[:], window[:], Act.Square)
+        nc.tensor.matmul(mean_square[:], mean_weights[:], squares[:], start=True, stop=True)
+        nc.scalar.activation(inverse_rms[:], mean_square[:], Act.Abs_reciprocal_sqrt, bias=eps[:])
+        nc.vector.scalar_tensor_tensor(result[:], window[:], gain[:], inverse_rms[:], mult, mult)
+        nc.sync.dma_start(out, result[:])

@@ -11,6 +11,7 @@ EXPERTS = 4
 PIECE = 64
 ENTRIES = EXPERTS * PIECE
 EPS = 1e-5
+HALVES = 2
 
 FLOPS = 2 * BLOCKS * P * P * (TOKENS + ENTRIES) + 4 * P * TOKENS
 
@@ -40,6 +41,9 @@ def tile_rows_placenorm_proj_kernel(tc, a, wd, x, w, s, offs, out):
         eps = held.tile([P, 1], F32)
         nc.vector.memset(eps[:], EPS)
 
+        table_warm_up = held.tile([P, 1], F32)
+        nc.scalar.activation(table_warm_up[:], eps[:], Act.Abs_reciprocal_sqrt, bias=eps[:])
+
         window = psum.tile([P, TOKENS], F32)
         for b in range(BLOCKS):
             nc.tensor.matmul(window[:], wd_tile[:, b, :], a_tile[:, b, :], start=(b == 0), stop=False)
@@ -56,11 +60,14 @@ def tile_rows_placenorm_proj_kernel(tc, a, wd, x, w, s, offs, out):
                 )
 
         squares = held.tile([P, TOKENS], BF16)
-        mean_square = psum.tile([P, TOKENS], F32)
         inverse_rms = held.tile([P, TOKENS], F32)
         result = held.tile([P, TOKENS], F32)
-        nc.scalar.activation(squares[:], window[:], Act.Square)
-        nc.tensor.matmul(mean_square[:], mean_weights[:], squares[:], start=True, stop=True)
-        nc.scalar.activation(inverse_rms[:], mean_square[:], Act.Abs_reciprocal_sqrt, bias=eps[:])
-        nc.vector.scalar_tensor_tensor(result[:], window[:], gain[:], inverse_rms[:], mult, mult)
-        nc.sync.dma_start(out, result[:])
+        halves = [slice(h * TOKENS // HALVES, (h + 1) * TOKENS // HALVES) for h in range(HALVES)]
+        mean_squares = [psum.tile([P, TOKENS // HALVES], F32, name=f"mean_square{h}") for h in range(HALVES)]
+        for half, mean_square in zip(halves, mean_squares):
+            nc.scalar.activation(squares[:, half], window[:, half], Act.Square)
+            nc.tensor.matmul(mean_square[:], mean_weights[:], squares[:, half], start=True, stop=True)
+        for half, mean_square in zip(halves, mean_squares):
+            nc.scalar.activation(inverse_rms[:, half], mean_square[:], Act.Abs_reciprocal_sqrt, bias=eps[:])
+            nc.vector.scalar_tensor_tensor(result[:, half], window[:, half], gain[:], inverse_rms[:, half], mult, mult)
+            nc.sync.dma_start(out[:, half], result[:, half])

@@ -11,6 +11,7 @@ EXPERTS = 4
 PIECE = 64
 ENTRIES = EXPERTS * PIECE
 EPS = 1e-5
+WARM_UPS = 4
 HALVES = 2
 
 FLOPS = 2 * BLOCKS * P * P * (TOKENS + ENTRIES) + 4 * P * TOKENS
@@ -40,6 +41,12 @@ def tile_rows_placenorm_proj_kernel(tc, a, wd, x, w, s, offs, out):
         nc.vector.memset(mean_weights[:], 1.0 / P)
         eps = held.tile([P, 1], F32)
         nc.vector.memset(eps[:], EPS)
+
+        zeros = held.tile([P, TOKENS], BF16)
+        nc.gpsimd.memset(zeros[:], 0.0)
+        unread = psum.tile([P, TOKENS], F32)
+        for turn in range(WARM_UPS):
+            nc.tensor.matmul(unread[:], zeros[:, 0:P], zeros[:], start=True, stop=True)
 
         table_warm_up = held.tile([P, 1], F32)
         nc.scalar.activation(table_warm_up[:], eps[:], Act.Abs_reciprocal_sqrt, bias=eps[:])

@@ -30,20 +30,20 @@ def tile_rows_placenorm_proj_kernel(tc, a, wd, x, w, s, offs, out):
         gain = held.tile([P, 1], F32)
         offsets = held.tile([P, ENTRIES // 16], U16)
 
+        nc.sync.dma_start(wd_tile[:], wd.rearrange("(p b) m -> p b m", b=BLOCKS))
         nc.sync.dma_start(a_tile[:], a.rearrange("(p b) i -> p b i", b=BLOCKS))
-        nc.scalar.dma_start(wd_tile[:], wd.rearrange("(p b) m -> p b m", b=BLOCKS))
         nc.sync.dma_start(offsets[:], offs)
-        nc.scalar.dma_start(w_tile[:], w.rearrange("e (p b) m -> p e b m", b=BLOCKS))
         nc.sync.dma_start(x_tile[:], x.rearrange("(p b) j -> p b j", b=BLOCKS))
-        nc.scalar.dma_start(gain[:], s)
+        nc.sync.dma_start(w_tile[:], w.rearrange("e (p b) m -> p e b m", b=BLOCKS))
+        nc.sync.dma_start(gain[:], s)
 
-        mean_weights = held.tile([P, P], BF16)
-        nc.vector.memset(mean_weights[:], 1.0 / P)
         eps = held.tile([P, 1], F32)
-        nc.vector.memset(eps[:], EPS)
+        nc.gpsimd.memset(eps[:], EPS)
+        mean_weights = held.tile([P, P], BF16)
+        nc.gpsimd.memset(mean_weights[:], 1.0 / P)
 
         zeros = held.tile([P, TOKENS], BF16)
-        nc.gpsimd.memset(zeros[:], 0.0)
+        nc.vector.memset(zeros[:], 0.0)
         unread = psum.tile([P, TOKENS], F32)
         for turn in range(WARM_UPS):
             nc.tensor.matmul(unread[:], zeros[:, 0:P], zeros[:], start=True, stop=True)

@@ -10,9 +10,13 @@ TOKENS = 512
 EXPERTS = 4
 PIECE = 64
 ENTRIES = EXPERTS * PIECE
+LIST_COLUMNS = PIECE // 16
 EPS = 1e-5
 WARM_UPS = 4
-HALVES = 2
+STORES = 2
+PARTS = 4
+PART = TOKENS // PARTS
+STORE = TOKENS // STORES
 
 FLOPS = 2 * BLOCKS * P * P * (TOKENS + ENTRIES) + 4 * P * TOKENS
 
@@ -23,12 +27,12 @@ def tile_rows_placenorm_proj_kernel(tc, a, wd, x, w, s, offs, out):
         tc.tile_pool(name="held", bufs=1) as held,
         tc.psum_pool(name="psum", bufs=1) as psum,
     ):
-        a_tile = held.tile([P, BLOCKS, TOKENS], BF16)
         wd_tile = held.tile([P, BLOCKS, P], BF16)
+        a_tile = held.tile([P, BLOCKS, TOKENS], BF16)
+        offsets = held.tile([P, ENTRIES // 16], U16)
         x_tile = held.tile([P, BLOCKS, ENTRIES], BF16)
         w_tile = held.tile([P, EXPERTS, BLOCKS, P], BF16)
         gain = held.tile([P, 1], F32)
-        offsets = held.tile([P, ENTRIES // 16], U16)
 
         nc.sync.dma_start(wd_tile[:], wd.rearrange("(p b) m -> p b m", b=BLOCKS))
         nc.sync.dma_start(a_tile[:], a.rearrange("(p b) i -> p b i", b=BLOCKS))
@@ -56,7 +60,7 @@ def tile_rows_placenorm_proj_kernel(tc, a, wd, x, w, s, offs, out):
             nc.tensor.matmul(window[:], wd_tile[:, b, :], a_tile[:, b, :], start=(b == 0), stop=False)
 
         for e in range(EXPERTS):
-            placed = window[:].indirect(offsets[:, e * PIECE // 16 : (e + 1) * PIECE // 16])
+            placed = window[:].indirect(offsets[:, e * LIST_COLUMNS : (e + 1) * LIST_COLUMNS])
             for b in range(BLOCKS):
                 nc.tensor.matmul(
                     placed,
@@ -69,12 +73,18 @@ def tile_rows_placenorm_proj_kernel(tc, a, wd, x, w, s, offs, out):
         squares = held.tile([P, TOKENS], BF16)
         inverse_rms = held.tile([P, TOKENS], F32)
         result = held.tile([P, TOKENS], F32)
-        halves = [slice(h * TOKENS // HALVES, (h + 1) * TOKENS // HALVES) for h in range(HALVES)]
-        mean_squares = [psum.tile([P, TOKENS // HALVES], F32, name=f"mean_square{h}") for h in range(HALVES)]
-        for half, mean_square in zip(halves, mean_squares):
-            nc.scalar.activation(squares[:, half], window[:, half], Act.Square)
-            nc.tensor.matmul(mean_square[:], mean_weights[:], squares[:, half], start=True, stop=True)
-        for half, mean_square in zip(halves, mean_squares):
-            nc.scalar.activation(inverse_rms[:, half], mean_square[:], Act.Abs_reciprocal_sqrt, bias=eps[:])
-            nc.vector.scalar_tensor_tensor(result[:, half], window[:, half], gain[:], inverse_rms[:, half], mult, mult)
+        mean_squares = [psum.tile([P, PART], F32, name=f"mean_square{q}") for q in range(PARTS)]
+        for q in range(PARTS):
+            part = slice(q * PART, (q + 1) * PART)
+            nc.scalar.activation(squares[:, part], window[:, part], Act.Square)
+            nc.tensor.matmul(mean_squares[q][:], mean_weights[:], squares[:, part], start=True, stop=True)
+
+        for h in range(STORES):
+            for q in range(h * PARTS // STORES, (h + 1) * PARTS // STORES):
+                part = slice(q * PART, (q + 1) * PART)
+                nc.scalar.activation(inverse_rms[:, part], mean_squares[q][:], Act.Abs_reciprocal_sqrt, bias=eps[:])
+                nc.vector.scalar_tensor_tensor(
+                    result[:, part], window[:, part], gain[:], inverse_rms[:, part], mult, mult
+                )
+            half = slice(h * STORE, (h + 1) * STORE)
             nc.sync.dma_start(out[:, half], result[:, half])

import concourse.mybir as mybir

BF16, F32, U16 = mybir.dt.bfloat16, mybir.dt.float32, mybir.dt.uint16
Act = mybir.ActivationFunctionType
mult = mybir.AluOpType.mult

P = 128
BLOCKS = 2
TOKENS = 512
EXPERTS = 4
PIECE = 64
ENTRIES = EXPERTS * PIECE
LIST_COLUMNS = PIECE // 16
EPS = 1e-5
WARM_UPS = 4
STORES = 2
PARTS = 4
PART = TOKENS // PARTS
STORE = TOKENS // STORES

FLOPS = 2 * BLOCKS * P * P * (TOKENS + ENTRIES) + 4 * P * TOKENS


def tile_rows_placenorm_proj_kernel(tc, a, wd, x, w, s, offs, out):
    nc = tc.nc
    with (
        tc.tile_pool(name="held", bufs=1) as held,
        tc.psum_pool(name="psum", bufs=1) as psum,
    ):
        wd_tile = held.tile([P, BLOCKS, P], BF16)
        a_tile = held.tile([P, BLOCKS, TOKENS], BF16)
        offsets = held.tile([P, ENTRIES // 16], U16)
        x_tile = held.tile([P, BLOCKS, ENTRIES], BF16)
        w_tile = held.tile([P, EXPERTS, BLOCKS, P], BF16)
        gain = held.tile([P, 1], F32)

        nc.sync.dma_start(wd_tile[:], wd.rearrange("(p b) m -> p b m", b=BLOCKS))
        nc.sync.dma_start(a_tile[:], a.rearrange("(p b) i -> p b i", b=BLOCKS))
        nc.sync.dma_start(offsets[:], offs)
        nc.sync.dma_start(x_tile[:], x.rearrange("(p b) j -> p b j", b=BLOCKS))
        nc.sync.dma_start(w_tile[:], w.rearrange("e (p b) m -> p e b m", b=BLOCKS))
        nc.sync.dma_start(gain[:], s)

        eps = held.tile([P, 1], F32)
        nc.gpsimd.memset(eps[:], EPS)
        mean_weights = held.tile([P, P], BF16)
        nc.gpsimd.memset(mean_weights[:], 1.0 / P)

        zeros = held.tile([P, TOKENS], BF16)
        nc.vector.memset(zeros[:], 0.0)
        unread = psum.tile([P, TOKENS], F32)
        for turn in range(WARM_UPS):
            nc.tensor.matmul(unread[:], zeros[:, 0:P], zeros[:], start=True, stop=True)

        table_warm_up = held.tile([P, 1], F32)
        nc.scalar.activation(table_warm_up[:], eps[:], Act.Abs_reciprocal_sqrt, bias=eps[:])

        window = psum.tile([P, TOKENS], F32)
        for b in range(BLOCKS):
            nc.tensor.matmul(window[:], wd_tile[:, b, :], a_tile[:, b, :], start=(b == 0), stop=False)

        for e in range(EXPERTS):
            placed = window[:].indirect(offsets[:, e * LIST_COLUMNS : (e + 1) * LIST_COLUMNS])
            for b in range(BLOCKS):
                nc.tensor.matmul(
                    placed,
                    w_tile[:, e, b, :],
                    x_tile[:, b, e * PIECE : (e + 1) * PIECE],
                    start=False,
                    stop=(e == EXPERTS - 1 and b == BLOCKS - 1),
                )

        squares = held.tile([P, TOKENS], BF16)
        inverse_rms = held.tile([P, TOKENS], F32)
        result = held.tile([P, TOKENS], F32)
        mean_squares = [psum.tile([P, PART], F32, name=f"mean_square{q}") for q in range(PARTS)]
        for q in range(PARTS):
            part = slice(q * PART, (q + 1) * PART)
            nc.scalar.activation(squares[:, part], window[:, part], Act.Square)
            nc.tensor.matmul(mean_squares[q][:], mean_weights[:], squares[:, part], start=True, stop=True)

        for h in range(STORES):
            for q in range(h * PARTS // STORES, (h + 1) * PARTS // STORES):
                part = slice(q * PART, (q + 1) * PART)
                nc.scalar.activation(inverse_rms[:, part], mean_squares[q][:], Act.Abs_reciprocal_sqrt, bias=eps[:])
                nc.vector.scalar_tensor_tensor(
                    result[:, part], window[:, part], gain[:], inverse_rms[:, part], mult, mult
                )
            half = slice(h * STORE, (h + 1) * STORE)
            nc.sync.dma_start(out[:, half], result[:, half])
